import numpy as np, ml_dtypes
CORES = [3,5,43,45,51,53,67,69,75,77,83,85,91,93,115,117]
N = 16
import mx_ref
NC, HD, G = 128, 2, 4
C, DEC = np.float32(0.047), np.float32(0.8)
BF = ml_dtypes.bfloat16
def cut(t, i, w=512):
    return t[:, w * i:w * i + w]
def tile(rs):
    return np.stack(rs, axis=2).reshape(128, -1).astype(BF)
def layer(w, X):
    out = []
    for i in range(G):
        for t in range(len(X)):
            p = mx_ref.matmul(mx_ref.quantize(cut(w, len(X) * i + t)), X[t])
            z = p if t == 0 else z + p
        out.append(z)
    return out
def pick(b):
    s = np.zeros((128, 128, 4), np.float32)
    s[np.arange(128), np.arange(128), b] = 1.0
    return mx_ref.quantize(s.reshape(128, 512).astype(BF))
def setup_inputs(rng):
    def f(*shape):
        return mx_ref.flush((rng.standard_normal(shape, dtype=np.float32) * np.exp2(rng.integers(-2, 3, shape[:-1] + (1,)))).astype(BF))
    return {"k": f(N, 128, HD * 4 * 512), "v": f(N, 128, HD * 512), "q": f(N, 128, HD * 4 * NC)}
def setup_inputs_blocks(rng):
    d = setup_inputs(rng)
    for k in ("k", "v", "q"): d[k] = mx_ref.spread(d[k], rng, 4)
    return d
def setup_inputs_wide(rng):
    d = setup_inputs(rng)
    for k in ("k", "v", "q"): d[k] = mx_ref.flush((d[k].astype(np.float32) * np.exp2(rng.integers(-4, 5, (N, 1, 1))).astype(np.float32)).astype(BF))
    return d
def setup_inputs_zeros(rng):
    d = setup_inputs(rng); v = d["v"].reshape(N, 128, -1, 4).copy()
    v[np.broadcast_to((rng.random((N, 1, v.shape[2], 1)) < 0.33), v.shape)] = 0
    d["v"] = v.reshape(d["v"].shape)
    return d
def reference(k, v, q):
    S = [pick(t) for t in range(4)]
    y = np.zeros((N, 128, HD * NC), np.float32)
    for a in range(HD):
        for r in range(N):
            R = [z * C for z in layer(cut(k[r], a, 4 * 512), [mx_ref.quantize(cut(v[r], a))])]
            if r > 0: R = [R[t] + mx_ref.matmul(S[t], s) * DEC for t in range(4)]
            s = mx_ref.quantize(tile(R))
            y[r][:, NC * a:NC * a + NC] = mx_ref.matmul(s, mx_ref.quantize(cut(q[r], a, 4 * NC)))
    return {"y": y}

@@ -1,0 +1,213 @@
+import numpy as np
+from concourse.mybir import dt, AluOpType, ActivationFunctionType
+
+N, HEADS, G, NC = 16, 2, 4, 128
+W = 4 * NC
+BANK = 512
+C = float(np.float32(0.047))
+DEC = float(np.float32(0.8))
+F8, U8, BF, F32 = "float8_e4m3fn_x4", "uint8", "bfloat16", "float32"
+
+SCRATCH = {
+    "kt": ("sbuf", [128, HEADS * G * W], BF), "vt": ("sbuf", [128, HEADS * W], BF), "qt": ("sbuf", [128, HEADS * W], BF),
+    "kc": ("sbuf", [128, HEADS * G * NC], F8), "kp": ("sbuf", [128, HEADS * G * NC], U8),
+    "vc": ("sbuf", [128, HEADS * NC], F8), "vp": ("sbuf", [128, HEADS * NC], U8),
+    "qc": ("sbuf", [128, HEADS * NC], F8), "qp": ("sbuf", [128, HEADS * NC], U8),
+    "one": ("sbuf", [128, W + 4], BF), "w": ("sbuf", [128, W + 4], BF),
+    "sc": ("sbuf", [128, G * NC], F8), "sp": ("sbuf", [128, G * NC], U8),
+    "zs": ("sbuf", [128, HEADS * G * NC], F32), "ds": ("sbuf", [128, HEADS * G * NC], F32),
+    "t0": ("sbuf", [128, W], BF), "t1": ("sbuf", [128, W], BF),
+    "oc": ("sbuf", [128, HEADS * NC], F8), "op": ("sbuf", [128, HEADS * NC], U8),
+    "ic": ("sbuf", [128, HEADS * NC], F8), "ip": ("sbuf", [128, HEADS * NC], U8),
+    "rc": ("sbuf", [128, HEADS * NC], F8), "rp": ("sbuf", [128, HEADS * NC], U8),
+    "ys": ("sbuf", [128, HEADS * NC], F32),
+    "ps": ("psum", [128, 8 * BANK], F32),
+}
+_A = ["lv", "lk", "lq", "qv", "qk", "qo", "ez", "at", "my", "ey", "cin", "pin", "crl", "prl"]
+SEMAPHORES = (["%s%d" % (n, a) for n in _A for a in range(HEADS)]
+              + ["%s%d" % (n, i) for n in ("mz", "md", "ed") for i in range(HEADS * G)]
+              + ["lk0%d" % i for i in range(G)] + ["qk0%d" % i for i in range(G)]
+              + ["one", "w", "qs", "qq", "st", "loc"])
+
+
+def engines(topo, src, dst):
+    m = topo.mask(src, dst)
+    bits = [i for i in range(m.bit_length()) if (m >> i) & 1]
+    step = max(1, len(bits) // 8)
+    return sum(1 << i for i in bits[::step])
+
+
+def count(mask):
+    return bin(mask).count("1")
+
+
+def way(T, topo, r):
+    src, dst = T.cores[r], T.cores[r + 1]
+    if topo.may_write(src, dst):
+        return None, None
+    chip = topo.chip(src)
+    near = [c for c in range(128) if c != src and topo.chip(c) == chip and topo.may_write(c, dst)]
+    idle = [c for c in near if T.rank_of(c) is None]
+    idle.sort(key=lambda c: (topo.die(c) != topo.die(src), c))
+    before = T.cores[r - 1] if r > 0 and T.cores[r - 1] in near else None
+    plane = before if before is not None else idle[-1]
+    codes = before if before is not None and r == 1 else idle[0]
+    return codes, plane
+
+
+def rank_program(g, core, T, topo):
+    sent = [0]
+    COPY = ActivationFunctionType.Copy
+
+    def sem(name):
+        return T.sem[name]
+
+    def cols(a):
+        return slice(NC * a, NC * a + NC)
+
+    def send(dst, out, in_, s):
+        rid, pid, _ = topo.addr(dst)
+        m = engines(topo, core, dst)
+        g.remote_dma(out, in_, sem(s), T.sem.loc, pid, rid, m)
+        sent[0] += count(m)
+
+    def codes(buf, a):
+        return T[buf][:, cols(a)].bitcast(dt.uint8)
+
+    def plane(buf, a):
+        return T[buf][:, cols(a)]
+
+    rank = T.rank_of(core)
+
+    if rank is not None:
+        def kt(a, i):
+            return slice(W * (G * a + i), W * (G * a + i) + W)
+        g.sync.dma_start(T.vt[:, 0:W], T.v[:, 0:W]).then_inc(T.sem.lv0, 16)
+        for i in range(G):
+            queue = g.sync if i % 2 else g.scalar
+            queue.dma_start(T.kt[:, kt(0, i)], T.k[:, kt(0, i)]).then_inc(sem("lk0%d" % i), 16)
+        g.sync.dma_start(T.vt[:, W:2 * W], T.v[:, W:2 * W]).then_inc(T.sem.lv1, 16)
+        g.sync.dma_start(T.kt[:, G * W:2 * G * W], T.k[:, G * W:2 * G * W]).then_inc(T.sem.lk1, 16)
+        g.sync.dma_start(T.qt[:], T.q[:]).then_inc(T.sem.lq0, 16)
+
+        def quantise_q():
+            g.vector.wait_ge(T.sem.lq0, 16)
+            g.vector.quantize_mx(T.qc[:], T.qp[:], T.qt[:]).then_inc(T.sem.qq, 1)
+
+        if rank > 0:
+            g.vector.memset(T.one[:], 1.0).then_inc(T.sem.one, 1)
+            g.wait_ge(T.sem.one, 1)
+            g.affine_select(T.w[:], T.one[:], [[-1, W + 4]], AluOpType.is_equal, 0.0, 3, 4).then_inc(T.sem.w, 1)
+        g.vector.wait_ge(T.sem.lv0, 16)
+        g.vector.quantize_mx(T.vc[:, cols(0)], T.vp[:, cols(0)], T.vt[:, 0:W]).then_inc(T.sem.qv0, 1)
+        for i in range(G):
+            g.vector.wait_ge(sem("lk0%d" % i), 16)
+            g.vector.quantize_mx(T.kc[:, cols(i)], T.kp[:, cols(i)], T.kt[:, kt(0, i)]).then_inc(sem("qk0%d" % i), 1)
+
+        def quantise_head1():
+            g.vector.wait_ge(T.sem.lv1, 16)
+            g.vector.quantize_mx(T.vc[:, cols(1)], T.vp[:, cols(1)], T.vt[:, W:2 * W]).then_inc(T.sem.qv1, 1)
+            g.vector.wait_ge(T.sem.lk1, 16)
+            g.vector.quantize_mx(T.kc[:, G * NC:2 * G * NC], T.kp[:, G * NC:2 * G * NC], T.kt[:, G * W:2 * G * W]).then_inc(T.sem.qk1, 1)
+
+        def quantise_state(a):
+            g.vector.wait_ge(sem("at%d" % a), G)
+            g.vector.quantize_mx(T.oc[:, cols(a)], T.op[:, cols(a)], T["t%d" % a][:]).then_inc(sem("qo%d" % a), 1)
+
+        if rank == 0:
+            quantise_state(0)
+            quantise_head1()
+            quantise_state(1)
+            quantise_q()
+        else:
+            g.vector.wait_ge(T.sem.w, 1)
+            for b in range(G):
+                g.vector.quantize_mx(T.sc[:, cols(b)], T.sp[:, cols(b)], T.w[:, 3 - b:3 - b + W]).then_inc(T.sem.qs, 1)
+            quantise_head1()
+            if rank > 1:
+                quantise_q()
+            g.vector.wait_ge(T.sem.ez0, G)
+            g.vector.wait_ge(T.sem.ez1, G)
+            for a in range(HEADS):
+                for b in range(G):
+                    i = G * a + b
+                    g.vector.wait_ge(sem("ed%d" % i), 1)
+                    g.vector.tensor_tensor(T["t%d" % a][:, b:W:G], T.ds[:, cols(i)], T.zs[:, cols(i)], AluOpType.add).then_inc(sem("at%d" % a), 1)
+                quantise_state(a)
+            if rank == 1:
+                quantise_q()
+
+        def bank(i):
+            return T.ps[:, BANK * i:BANK * i + NC]
+        for a in range(HEADS):
+            g.tensor.wait_ge(sem("qv%d" % a), 1)
+            if a == 1:
+                g.tensor.wait_ge(T.sem.qk1, 1)
+            for b in range(G):
+                i = G * a + b
+                if a == 0:
+                    g.tensor.wait_ge(sem("qk0%d" % b), 1)
+                g.tensor.matmul_mx(bank(i), T.kc[:, cols(i)], T.kp[:, cols(i)], T.vc[:, cols(a)], T.vp[:, cols(a)], True, True).then_inc(sem("mz%d" % i), 1)
+        if rank > 0:
+            g.tensor.wait_ge(T.sem.qs, G)
+            for a in range(HEADS):
+                g.tensor.wait_ge(sem("ez%d" % a), G)
+            for a in range(HEADS):
+                prev = T.cores[rank - 1]
+                rc, rp = way(T, topo, rank - 1)
+                g.tensor.wait_ge(sem("cin%d" % a), count(engines(topo, rc if rc is not None else prev, core)))
+                g.tensor.wait_ge(sem("pin%d" % a), count(engines(topo, rp if rp is not None else prev, core)))
+                for b in range(G):
+                    i = G * a + b
+                    g.tensor.matmul_mx(bank(i), T.sc[:, cols(b)], T.sp[:, cols(b)], T.ic[:, cols(a)], T.ip[:, cols(a)], True, True).then_inc(sem("md%d" % i), 1)
+        for a in range(HEADS):
+            g.tensor.wait_ge(sem("qo%d" % a), 1)
+            if a == 0:
+                g.tensor.wait_ge(T.sem.qq, 1)
+            g.tensor.matmul_mx(bank(a), T.oc[:, cols(a)], T.op[:, cols(a)], T.qc[:, cols(a)], T.qp[:, cols(a)], True, True).then_inc(sem("my%d" % a), 1)
+
+        for a in range(HEADS):
+            for b in range(G):
+                i = G * a + b
+                g.scalar.wait_ge(sem("mz%d" % i), 1)
+                if rank == 0:
+                    g.scalar.activation(T["t%d" % a][:, b:W:G], bank(i), COPY, scale=C).then_inc(sem("at%d" % a), 1)
+                else:
+                    g.scalar.activation(T.zs[:, cols(i)], bank(i), COPY, scale=C).then_inc(sem("ez%d" % a), 1)
+        if rank > 0:
+            for i in range(HEADS * G):
+                g.scalar.wait_ge(sem("md%d" % i), 1)
+                g.scalar.activation(T.ds[:, cols(i)], bank(i), COPY, scale=DEC).then_inc(sem("ed%d" % i), 1)
+        for a in range(HEADS):
+            g.scalar.wait_ge(sem("my%d" % a), 1)
+            g.scalar.activation(T.ys[:, cols(a)], bank(a), COPY).then_inc(sem("ey%d" % a), 1)
+
+        for a in range(HEADS):
+            g.sync.wait_ge(sem("ey%d" % a), 1)
+            g.sync.dma_start(T.y[:, cols(a)], T.ys[:, cols(a)]).then_inc(T.sem.st, 16)
+        g.sync.wait_ge(T.sem.st, 16 * HEADS)
+
+        if rank < N - 1:
+            rc, rp = way(T, topo, rank)
+            for a in range(HEADS):
+                g.wait_ge(sem("qo%d" % a), 1)
+                if rc is None:
+                    send(T.cores[rank + 1], codes("ic", a), codes("oc", a), "cin%d" % a)
+                else:
+                    send(rc, codes("rc", a), codes("oc", a), "crl%d" % a)
+                if rp is None:
+                    send(T.cores[rank + 1], plane("ip", a), plane("op", a), "pin%d" % a)
+                else:
+                    send(rp, plane("rp", a), plane("op", a), "prl%d" % a)
+
+    for r in range(N - 1):
+        rc, rp = way(T, topo, r)
+        for a in range(HEADS):
+            if rc == core:
+                g.wait_ge(sem("crl%d" % a), count(engines(topo, T.cores[r], core)))
+                send(T.cores[r + 1], codes("ic", a), codes("rc", a), "cin%d" % a)
+            if rp == core:
+                g.wait_ge(sem("prl%d" % a), count(engines(topo, T.cores[r], core)))
+                send(T.cores[r + 1], plane("ip", a), plane("rp", a), "pin%d" % a)
+    if sent[0]:
+        g.wait_ge(T.sem.loc, sent[0])

@@ -7,6 +7,7 @@ BANK = 512
 C = float(np.float32(0.047))
 DEC = float(np.float32(0.8))
 F8, U8, BF, F32 = "float8_e4m3fn_x4", "uint8", "bfloat16", "float32"
+SLOTS = 3
 
 SCRATCH = {
     "kt": ("sbuf", [128, HEADS * G * W], BF), "vt": ("sbuf", [128, HEADS * W], BF), "qt": ("sbuf", [128, HEADS * W], BF),
@@ -19,45 +20,66 @@ SCRATCH = {
     "t0": ("sbuf", [128, W], BF), "t1": ("sbuf", [128, W], BF),
     "oc": ("sbuf", [128, HEADS * NC], F8), "op": ("sbuf", [128, HEADS * NC], U8),
     "ic": ("sbuf", [128, HEADS * NC], F8), "ip": ("sbuf", [128, HEADS * NC], U8),
-    "rc": ("sbuf", [128, HEADS * NC], F8), "rp": ("sbuf", [128, HEADS * NC], U8),
+    "rc": ("sbuf", [128, SLOTS * NC], F8), "rp": ("sbuf", [128, SLOTS * NC], U8),
     "ys": ("sbuf", [128, HEADS * NC], F32),
     "ps": ("psum", [128, 8 * BANK], F32),
 }
-_A = ["lv", "lk", "lq", "qv", "qk", "qo", "ez", "at", "my", "ey", "cin", "pin", "crl", "prl"]
+_A = ["lv", "qv", "qo", "ez", "at", "my", "ey", "cin", "pin"]
 SEMAPHORES = (["%s%d" % (n, a) for n in _A for a in range(HEADS)]
               + ["%s%d" % (n, i) for n in ("mz", "md", "ed") for i in range(HEADS * G)]
               + ["lk0%d" % i for i in range(G)] + ["qk0%d" % i for i in range(G)]
-              + ["one", "w", "qs", "qq", "st", "loc"])
+              + ["%s%d" % (n, i) for n in ("crl", "prl") for i in range(SLOTS)]
+              + ["lk1", "lq", "qk1", "one", "w", "qs", "qq", "st", "loc"])
 
 
-def engines(topo, src, dst):
+def engines(topo, src, dst, kind):
     m = topo.mask(src, dst)
     bits = [i for i in range(m.bit_length()) if (m >> i) & 1]
     step = max(1, len(bits) // 8)
-    return sum(1 << i for i in bits[::step])
+    first = step - 1 if kind == "p" else 0
+    return sum(1 << i for i in bits[first::step])
 
 
 def count(mask):
     return bin(mask).count("1")
 
 
-def way(T, topo, r):
-    src, dst = T.cores[r], T.cores[r + 1]
-    if topo.may_write(src, dst):
-        return None, None
-    chip = topo.chip(src)
-    near = [c for c in range(128) if c != src and topo.chip(c) == chip and topo.may_write(c, dst)]
-    idle = [c for c in near if T.rank_of(c) is None]
-    idle.sort(key=lambda c: (topo.die(c) != topo.die(src), c))
-    before = T.cores[r - 1] if r > 0 and T.cores[r - 1] in near else None
-    plane = before if before is not None else idle[-1]
-    codes = before if before is not None and r == 1 else idle[0]
-    return codes, plane
+def routes(T, topo):
+    cores = T.cores
+    crossing = [r for r in range(N - 1) if not topo.may_write(cores[r], cores[r + 1])]
+
+    def near(r):
+        src, dst = cores[r], cores[r + 1]
+        idle = [c for c in range(128) if topo.chip(c) == topo.chip(src) and topo.may_write(c, dst) and T.rank_of(c) is None]
+        return min(idle, key=lambda c: (topo.die(c) != topo.die(src), c))
+
+    def plane(r, s):
+        return topo.same_plane(topo.chip(cores[r]), topo.chip(cores[s]))
+
+    out, used = {}, []
+    for r in crossing:
+        before = cores[r - 1]
+        out[r, 0] = {"c": before if r == 1 else near(r), "p": before}
+        later = [s for s in crossing if s > r and plane(r, s)]
+        if later:
+            ahead = [cores[s] for s in range(r + 3, N - 1) if plane(r, s) and topo.may_write(cores[s], cores[r + 1]) and cores[s] not in used]
+            used.append(ahead[0])
+            out[r, 1] = {"c": near(later[0]), "p": ahead[0]}
+        else:
+            earlier = [s for s in crossing if s < r and plane(r, s)]
+            out[r, 1] = {"c": near(r), "p": near(earlier[-1])}
+    return out
 
 
 def rank_program(g, core, T, topo):
     sent = [0]
     COPY = ActivationFunctionType.Copy
+    ways = routes(T, topo)
+    rank = T.rank_of(core)
+    passing = {}
+    for key in sorted(ways):
+        for kind in ("c", "p"):
+            passing.setdefault((ways[key][kind], kind), []).append(key)
 
     def sem(name):
         return T.sem[name]
@@ -65,19 +87,32 @@ def rank_program(g, core, T, topo):
     def cols(a):
         return slice(NC * a, NC * a + NC)
 
-    def send(dst, out, in_, s):
+    def part(buf, kind, a):
+        v = T[buf + kind][:, cols(a)]
+        return v.bitcast(dt.uint8) if kind == "c" else v
+
+    def send(dst, kind, to, slot, buf, a, s):
         rid, pid, _ = topo.addr(dst)
-        m = engines(topo, core, dst)
-        g.remote_dma(out, in_, sem(s), T.sem.loc, pid, rid, m)
+        m = engines(topo, core, dst, kind)
+        g.remote_dma(part(to, kind, slot), part(buf, kind, a), sem(s), T.sem.loc, pid, rid, m)
         sent[0] += count(m)
 
-    def codes(buf, a):
-        return T[buf][:, cols(a)].bitcast(dt.uint8)
+    def hand_on(r, a):
+        g.wait_ge(sem("qo%d" % a), 1)
+        for kind in ("c", "p"):
+            if (r, a) in ways:
+                f = ways[r, a][kind]
+                slot = passing[f, kind].index((r, a))
+                send(f, kind, "r", slot, "o", a, "%srl%d" % (kind, slot))
+            else:
+                send(T.cores[r + 1], kind, "i", a, "o", a, "%sin%d" % (kind, a))
 
-    def plane(buf, a):
-        return T[buf][:, cols(a)]
-
-    rank = T.rank_of(core)
+    def forward(r, a):
+        for kind in ("c", "p"):
+            if (r, a) in passing.get((core, kind), []):
+                slot = passing[core, kind].index((r, a))
+                g.wait_ge(sem("%srl%d" % (kind, slot)), count(engines(topo, T.cores[r], core, kind)))
+                send(T.cores[r + 1], kind, "i", a, "r", slot, "%sin%d" % (kind, a))
 
     if rank is not None:
         def kt(a, i):
@@ -88,10 +123,10 @@ def rank_program(g, core, T, topo):
             queue.dma_start(T.kt[:, kt(0, i)], T.k[:, kt(0, i)]).then_inc(sem("lk0%d" % i), 16)
         g.sync.dma_start(T.vt[:, W:2 * W], T.v[:, W:2 * W]).then_inc(T.sem.lv1, 16)
         g.sync.dma_start(T.kt[:, G * W:2 * G * W], T.k[:, G * W:2 * G * W]).then_inc(T.sem.lk1, 16)
-        g.sync.dma_start(T.qt[:], T.q[:]).then_inc(T.sem.lq0, 16)
+        g.sync.dma_start(T.qt[:], T.q[:]).then_inc(T.sem.lq, 16)
 
         def quantise_q():
-            g.vector.wait_ge(T.sem.lq0, 16)
+            g.vector.wait_ge(T.sem.lq, 16)
             g.vector.quantize_mx(T.qc[:], T.qp[:], T.qt[:]).then_inc(T.sem.qq, 1)
 
         if rank > 0:
@@ -153,10 +188,9 @@ def rank_program(g, core, T, topo):
             for a in range(HEADS):
                 g.tensor.wait_ge(sem("ez%d" % a), G)
             for a in range(HEADS):
-                prev = T.cores[rank - 1]
-                rc, rp = way(T, topo, rank - 1)
-                g.tensor.wait_ge(sem("cin%d" % a), count(engines(topo, rc if rc is not None else prev, core)))
-                g.tensor.wait_ge(sem("pin%d" % a), count(engines(topo, rp if rp is not None else prev, core)))
+                for kind in ("c", "p"):
+                    last = ways[rank - 1, a][kind] if (rank - 1, a) in ways else T.cores[rank - 1]
+                    g.tensor.wait_ge(sem("%sin%d" % (kind, a)), count(engines(topo, last, core, kind)))
                 for b in range(G):
                     i = G * a + b
                     g.tensor.matmul_mx(bank(i), T.sc[:, cols(b)], T.sp[:, cols(b)], T.ic[:, cols(a)], T.ip[:, cols(a)], True, True).then_inc(sem("md%d" % i), 1)
@@ -187,27 +221,11 @@ def rank_program(g, core, T, topo):
             g.sync.dma_start(T.y[:, cols(a)], T.ys[:, cols(a)]).then_inc(T.sem.st, 16)
         g.sync.wait_ge(T.sem.st, 16 * HEADS)
 
-        if rank < N - 1:
-            rc, rp = way(T, topo, rank)
-            for a in range(HEADS):
-                g.wait_ge(sem("qo%d" % a), 1)
-                if rc is None:
-                    send(T.cores[rank + 1], codes("ic", a), codes("oc", a), "cin%d" % a)
-                else:
-                    send(rc, codes("rc", a), codes("oc", a), "crl%d" % a)
-                if rp is None:
-                    send(T.cores[rank + 1], plane("ip", a), plane("op", a), "pin%d" % a)
-                else:
-                    send(rp, plane("rp", a), plane("op", a), "prl%d" % a)
-
     for r in range(N - 1):
-        rc, rp = way(T, topo, r)
         for a in range(HEADS):
-            if rc == core:
-                g.wait_ge(sem("crl%d" % a), count(engines(topo, T.cores[r], core)))
-                send(T.cores[r + 1], codes("ic", a), codes("rc", a), "cin%d" % a)
-            if rp == core:
-                g.wait_ge(sem("prl%d" % a), count(engines(topo, T.cores[r], core)))
-                send(T.cores[r + 1], plane("ip", a), plane("rp", a), "pin%d" % a)
+            if r == rank:
+                hand_on(r, a)
+            else:
+                forward(r, a)
     if sent[0]:
         g.wait_ge(T.sem.loc, sent[0])

@@ -7,7 +7,9 @@ BANK = 512
 C = float(np.float32(0.047))
 DEC = float(np.float32(0.8))
 F8, U8, BF, F32 = "float8_e4m3fn_x4", "uint8", "bfloat16", "float32"
-SLOTS = 3
+ROOM = 3 * NC
+PLACES = 4
+RUNS = {4: (48, 40, 24, 16), 2: (64, 64)}
 
 SCRATCH = {
     "kt": ("sbuf", [128, HEADS * G * W], BF), "vt": ("sbuf", [128, HEADS * W], BF), "qt": ("sbuf", [128, HEADS * W], BF),
@@ -20,24 +22,25 @@ SCRATCH = {
     "t0": ("sbuf", [128, W], BF), "t1": ("sbuf", [128, W], BF),
     "oc": ("sbuf", [128, HEADS * NC], F8), "op": ("sbuf", [128, HEADS * NC], U8),
     "ic": ("sbuf", [128, HEADS * NC], F8), "ip": ("sbuf", [128, HEADS * NC], U8),
-    "rc": ("sbuf", [128, SLOTS * NC], F8), "rp": ("sbuf", [128, SLOTS * NC], U8),
+    "rc": ("sbuf", [128, ROOM], F8), "rp": ("sbuf", [128, ROOM], U8),
     "ys": ("sbuf", [128, HEADS * NC], F32),
     "ps": ("psum", [128, 8 * BANK], F32),
 }
-_A = ["lv", "qv", "qo", "ez", "at", "my", "ey", "cin", "pin"]
+_A = ["lv", "qv", "qo", "ez", "at", "my", "ey", "cin", "pin", "half"]
 SEMAPHORES = (["%s%d" % (n, a) for n in _A for a in range(HEADS)]
               + ["%s%d" % (n, i) for n in ("mz", "md", "ed") for i in range(HEADS * G)]
               + ["lk0%d" % i for i in range(G)] + ["qk0%d" % i for i in range(G)]
-              + ["%s%d" % (n, i) for n in ("crl", "prl") for i in range(SLOTS)]
-              + ["lk1", "lq", "qk1", "one", "w", "qs", "qq", "st", "loc"])
+              + ["lk1%d" % i for i in range(2)] + ["qk1%d" % i for i in range(2)]
+              + ["pass%d" % i for i in range(PLACES)]
+              + ["lq", "one", "w", "qs", "qq", "st", "loc"])
 
 
-def engines(topo, src, dst, kind):
+def engines(topo, src, dst, share):
     m = topo.mask(src, dst)
     bits = [i for i in range(m.bit_length()) if (m >> i) & 1]
-    step = max(1, len(bits) // 8)
-    first = step - 1 if kind == "p" else 0
-    return sum(1 << i for i in bits[first::step])
+    if share and len(bits) > 8:
+        bits = bits[0::2] if share == "c" else bits[1::2]
+    return sum(1 << i for i in bits)
 
 
 def count(mask):
@@ -56,19 +59,34 @@ def routes(T, topo):
     def plane(r, s):
         return topo.same_plane(topo.chip(cores[r]), topo.chip(cores[s]))
 
-    out, used = {}, []
-    for r in crossing:
-        before = cores[r - 1]
-        out[r, 0] = {"c": before if r == 1 else near(r), "p": before}
-        later = [s for s in crossing if s > r and plane(r, s)]
-        if later:
-            ahead = [cores[s] for s in range(r + 3, N - 1) if plane(r, s) and topo.may_write(cores[s], cores[r + 1]) and cores[s] not in used]
-            used.append(ahead[0])
-            out[r, 1] = {"c": near(later[0]), "p": ahead[0]}
-        else:
-            earlier = [s for s in crossing if s < r and plane(r, s)]
-            out[r, 1] = {"c": near(r), "p": near(earlier[-1])}
+    out = {}
+    for r in range(N - 1):
+        for a in range(HEADS):
+            if r not in crossing:
+                out[r, a] = [("c", 0, NC, (), ""), ("p", 0, NC, (), "")]
+                continue
+            before, share = cores[r - 1], a == 0
+            codes = before if r == crossing[0] else near(r)
+            out[r, a] = [("c", 0, NC, (codes,), "c" if share else ""), ("p", 0, NC, (before,), "p" if share else "")]
+        if r in crossing and not [s for s in crossing if s < r and plane(r, s)]:
+            later = [s for s in crossing if s > r and plane(r, s)]
+            ahead = [cores[s] for s in range(r + 3, N - 1) if plane(r, s) and topo.may_write(cores[s], cores[r + 1])]
+            there = [cores[s] for s in crossing if s > r and plane(r + 1, s)]
+            half = NC // 2
+            pieces = [("p", half * i, half, (ahead[i], there[i]), "") for i in range(2)]
+            by = []
+            for i in range(2):
+                by += [near(later[i])] + ahead[2:][::-1][i:i + 1]
+            first = 0
+            for f, n in zip(by, RUNS[len(by)]):
+                pieces.append(("c", first, n, (f,), ""))
+                first += n
+            out[r, 1] = pieces
     return out
+
+
+def parts(b):
+    return [(0, NC // 2), (NC // 2, NC // 2)] if b == 0 else [(0, NC)]
 
 
 def rank_program(g, core, T, topo):
@@ -76,10 +94,13 @@ def rank_program(g, core, T, topo):
     COPY = ActivationFunctionType.Copy
     ways = routes(T, topo)
     rank = T.rank_of(core)
-    passing = {}
+    passing, fill = {}, {}
     for key in sorted(ways):
-        for kind in ("c", "p"):
-            passing.setdefault((ways[key][kind], kind), []).append(key)
+        for j, (kind, first, n, by, share) in enumerate(ways[key]):
+            for f in by:
+                passing[f, key, j] = (fill.get(f, 0), fill.get((f, kind), 0))
+                fill[f] = fill.get(f, 0) + 1
+                fill[f, kind] = fill.get((f, kind), 0) + n
 
     def sem(name):
         return T.sem[name]
@@ -87,42 +108,54 @@ def rank_program(g, core, T, topo):
     def cols(a):
         return slice(NC * a, NC * a + NC)
 
-    def part(buf, kind, a):
-        v = T[buf + kind][:, cols(a)]
+    def view(buf, kind, first, n):
+        v = T[buf + kind][:, first:first + n]
         return v.bitcast(dt.uint8) if kind == "c" else v
 
-    def send(dst, kind, to, slot, buf, a, s):
+    def stations(key, j):
+        return [T.cores[key[0]]] + list(ways[key][j][3]) + [T.cores[key[0] + 1]]
+
+    def write(key, j, step, buf, at):
+        r, a = key
+        kind, first, n, by, share = ways[key][j]
+        dst = stations(key, j)[step + 1]
+        if step < len(by):
+            place, column = passing[dst, key, j]
+            to, s = view("r", kind, column, n), "pass%d" % place
+        else:
+            to, s = view("i", kind, NC * a + first, n), "%sin%d" % (kind, a)
         rid, pid, _ = topo.addr(dst)
-        m = engines(topo, core, dst, kind)
-        g.remote_dma(part(to, kind, slot), part(buf, kind, a), sem(s), T.sem.loc, pid, rid, m)
+        m = engines(topo, core, dst, share)
+        g.remote_dma(to, view(buf, kind, at, n), sem(s), T.sem.loc, pid, rid, m)
         sent[0] += count(m)
 
-    def hand_on(r, a):
-        g.wait_ge(sem("qo%d" % a), 1)
-        for kind in ("c", "p"):
-            if (r, a) in ways:
-                f = ways[r, a][kind]
-                slot = passing[f, kind].index((r, a))
-                send(f, kind, "r", slot, "o", a, "%srl%d" % (kind, slot))
-            else:
-                send(T.cores[r + 1], kind, "i", a, "o", a, "%sin%d" % (kind, a))
+    def hand_on(key):
+        g.wait_ge(sem("qo%d" % key[1]), 1)
+        for j, piece in enumerate(ways[key]):
+            write(key, j, 0, "o", NC * key[1] + piece[1])
 
-    def forward(r, a):
-        for kind in ("c", "p"):
-            if (r, a) in passing.get((core, kind), []):
-                slot = passing[core, kind].index((r, a))
-                g.wait_ge(sem("%srl%d" % (kind, slot)), count(engines(topo, T.cores[r], core, kind)))
-                send(T.cores[r + 1], kind, "i", a, "r", slot, "%sin%d" % (kind, a))
+    def forward(key):
+        for j, piece in enumerate(ways[key]):
+            if core in piece[3]:
+                step = piece[3].index(core) + 1
+                place, column = passing[core, key, j]
+                g.wait_ge(sem("pass%d" % place), count(engines(topo, stations(key, j)[step - 1], core, piece[4])))
+                write(key, j, step, "r", column)
+
+    def arriving(key, kind):
+        return sum(count(engines(topo, stations(key, j)[-2], core, p[4])) for j, p in enumerate(ways[key]) if p[0] == kind)
 
     if rank is not None:
-        def kt(a, i):
-            return slice(W * (G * a + i), W * (G * a + i) + W)
+        def kt(i, n=1):
+            return slice(W * i, W * (i + n))
         g.sync.dma_start(T.vt[:, 0:W], T.v[:, 0:W]).then_inc(T.sem.lv0, 16)
         for i in range(G):
             queue = g.sync if i % 2 else g.scalar
-            queue.dma_start(T.kt[:, kt(0, i)], T.k[:, kt(0, i)]).then_inc(sem("lk0%d" % i), 16)
+            queue.dma_start(T.kt[:, kt(i)], T.k[:, kt(i)]).then_inc(sem("lk0%d" % i), 16)
         g.sync.dma_start(T.vt[:, W:2 * W], T.v[:, W:2 * W]).then_inc(T.sem.lv1, 16)
-        g.sync.dma_start(T.kt[:, G * W:2 * G * W], T.k[:, G * W:2 * G * W]).then_inc(T.sem.lk1, 16)
+        for i in range(2):
+            queue = g.sync if i % 2 else g.scalar
+            queue.dma_start(T.kt[:, kt(G + 2 * i, 2)], T.k[:, kt(G + 2 * i, 2)]).then_inc(sem("lk1%d" % i), 16)
         g.sync.dma_start(T.qt[:], T.q[:]).then_inc(T.sem.lq, 16)
 
         def quantise_q():
@@ -137,22 +170,24 @@ def rank_program(g, core, T, topo):
         g.vector.quantize_mx(T.vc[:, cols(0)], T.vp[:, cols(0)], T.vt[:, 0:W]).then_inc(T.sem.qv0, 1)
         for i in range(G):
             g.vector.wait_ge(sem("lk0%d" % i), 16)
-            g.vector.quantize_mx(T.kc[:, cols(i)], T.kp[:, cols(i)], T.kt[:, kt(0, i)]).then_inc(sem("qk0%d" % i), 1)
+            g.vector.quantize_mx(T.kc[:, cols(i)], T.kp[:, cols(i)], T.kt[:, kt(i)]).then_inc(sem("qk0%d" % i), 1)
 
         def quantise_head1():
             g.vector.wait_ge(T.sem.lv1, 16)
             g.vector.quantize_mx(T.vc[:, cols(1)], T.vp[:, cols(1)], T.vt[:, W:2 * W]).then_inc(T.sem.qv1, 1)
-            g.vector.wait_ge(T.sem.lk1, 16)
-            g.vector.quantize_mx(T.kc[:, G * NC:2 * G * NC], T.kp[:, G * NC:2 * G * NC], T.kt[:, G * W:2 * G * W]).then_inc(T.sem.qk1, 1)
+            for i in range(2):
+                two = slice(NC * (G + 2 * i), NC * (G + 2 * i + 2))
+                g.vector.wait_ge(sem("lk1%d" % i), 16)
+                g.vector.quantize_mx(T.kc[:, two], T.kp[:, two], T.kt[:, kt(G + 2 * i, 2)]).then_inc(sem("qk1%d" % i), 1)
 
-        def quantise_state(a):
-            g.vector.wait_ge(sem("at%d" % a), G)
+        def quantise_state(a, n):
+            g.vector.wait_ge(sem("at%d" % a), n)
             g.vector.quantize_mx(T.oc[:, cols(a)], T.op[:, cols(a)], T["t%d" % a][:]).then_inc(sem("qo%d" % a), 1)
 
         if rank == 0:
-            quantise_state(0)
+            quantise_state(0, G)
             quantise_head1()
-            quantise_state(1)
+            quantise_state(1, G)
             quantise_q()
         else:
             g.vector.wait_ge(T.sem.w, 1)
@@ -164,24 +199,28 @@ def rank_program(g, core, T, topo):
             g.vector.wait_ge(T.sem.ez0, G)
             g.vector.wait_ge(T.sem.ez1, G)
             for a in range(HEADS):
+                made = 0
                 for b in range(G):
                     i = G * a + b
-                    g.vector.wait_ge(sem("ed%d" % i), 1)
-                    g.vector.tensor_tensor(T["t%d" % a][:, b:W:G], T.ds[:, cols(i)], T.zs[:, cols(i)], AluOpType.add).then_inc(sem("at%d" % a), 1)
-                quantise_state(a)
+                    for first, n in parts(b):
+                        g.vector.wait_ge(sem("half%d" % a if n < NC and first == 0 else "ed%d" % i), 1)
+                        x = slice(NC * i + first, NC * i + first + n)
+                        g.vector.tensor_tensor(T["t%d" % a][:, G * first + b:G * (first + n):G], T.ds[:, x], T.zs[:, x], AluOpType.add).then_inc(sem("at%d" % a), 1)
+                        made += 1
+                quantise_state(a, made)
             if rank == 1:
                 quantise_q()
 
-        def bank(i):
-            return T.ps[:, BANK * i:BANK * i + NC]
+        def bank(i, first=0, n=NC):
+            return T.ps[:, BANK * i + first:BANK * i + first + n]
         for a in range(HEADS):
             g.tensor.wait_ge(sem("qv%d" % a), 1)
-            if a == 1:
-                g.tensor.wait_ge(T.sem.qk1, 1)
             for b in range(G):
                 i = G * a + b
                 if a == 0:
                     g.tensor.wait_ge(sem("qk0%d" % b), 1)
+                elif b % 2 == 0:
+                    g.tensor.wait_ge(sem("qk1%d" % (b // 2)), 1)
                 g.tensor.matmul_mx(bank(i), T.kc[:, cols(i)], T.kp[:, cols(i)], T.vc[:, cols(a)], T.vp[:, cols(a)], True, True).then_inc(sem("mz%d" % i), 1)
         if rank > 0:
             g.tensor.wait_ge(T.sem.qs, G)
@@ -189,8 +228,7 @@ def rank_program(g, core, T, topo):
                 g.tensor.wait_ge(sem("ez%d" % a), G)
             for a in range(HEADS):
                 for kind in ("c", "p"):
-                    last = ways[rank - 1, a][kind] if (rank - 1, a) in ways else T.cores[rank - 1]
-                    g.tensor.wait_ge(sem("%sin%d" % (kind, a)), count(engines(topo, last, core, kind)))
+                    g.tensor.wait_ge(sem("%sin%d" % (kind, a)), arriving((rank - 1, a), kind))
                 for b in range(G):
                     i = G * a + b
                     g.tensor.matmul_mx(bank(i), T.sc[:, cols(b)], T.sp[:, cols(b)], T.ic[:, cols(a)], T.ip[:, cols(a)], True, True).then_inc(sem("md%d" % i), 1)
@@ -209,9 +247,13 @@ def rank_program(g, core, T, topo):
                 else:
                     g.scalar.activation(T.zs[:, cols(i)], bank(i), COPY, scale=C).then_inc(sem("ez%d" % a), 1)
         if rank > 0:
-            for i in range(HEADS * G):
-                g.scalar.wait_ge(sem("md%d" % i), 1)
-                g.scalar.activation(T.ds[:, cols(i)], bank(i), COPY, scale=DEC).then_inc(sem("ed%d" % i), 1)
+            for a in range(HEADS):
+                for b in range(G):
+                    i = G * a + b
+                    g.scalar.wait_ge(sem("md%d" % i), 1)
+                    for first, n in parts(b):
+                        done = sem("half%d" % a if n < NC and first == 0 else "ed%d" % i)
+                        g.scalar.activation(T.ds[:, NC * i + first:NC * i + first + n], bank(i, first, n), COPY, scale=DEC).then_inc(done, 1)
         for a in range(HEADS):
             g.scalar.wait_ge(sem("my%d" % a), 1)
             g.scalar.activation(T.ys[:, cols(a)], bank(a), COPY).then_inc(sem("ey%d" % a), 1)
@@ -221,11 +263,10 @@ def rank_program(g, core, T, topo):
             g.sync.dma_start(T.y[:, cols(a)], T.ys[:, cols(a)]).then_inc(T.sem.st, 16)
         g.sync.wait_ge(T.sem.st, 16 * HEADS)
 
-    for r in range(N - 1):
-        for a in range(HEADS):
-            if r == rank:
-                hand_on(r, a)
-            else:
-                forward(r, a)
+    for key in sorted(ways):
+        if key[0] == rank:
+            hand_on(key)
+        else:
+            forward(key)
     if sent[0]:
         g.wait_ge(T.sem.loc, sent[0])

import numpy as np
from concourse.mybir import dt, AluOpType, ActivationFunctionType

N, HEADS, G, NC = 16, 2, 4, 128
W = 4 * NC
BANK = 512
C = float(np.float32(0.047))
DEC = float(np.float32(0.8))
F8, U8, BF, F32 = "float8_e4m3fn_x4", "uint8", "bfloat16", "float32"
ROOM = 3 * NC
PLACES = 4
RUNS = {4: (48, 40, 24, 16), 2: (64, 64)}

SCRATCH = {
    "kt": ("sbuf", [128, HEADS * G * W], BF), "vt": ("sbuf", [128, HEADS * W], BF), "qt": ("sbuf", [128, HEADS * W], BF),
    "kc": ("sbuf", [128, HEADS * G * NC], F8), "kp": ("sbuf", [128, HEADS * G * NC], U8),
    "vc": ("sbuf", [128, HEADS * NC], F8), "vp": ("sbuf", [128, HEADS * NC], U8),
    "qc": ("sbuf", [128, HEADS * NC], F8), "qp": ("sbuf", [128, HEADS * NC], U8),
    "one": ("sbuf", [128, W + 4], BF), "w": ("sbuf", [128, W + 4], BF),
    "sc": ("sbuf", [128, G * NC], F8), "sp": ("sbuf", [128, G * NC], U8),
    "zs": ("sbuf", [128, HEADS * G * NC], F32), "ds": ("sbuf", [128, HEADS * G * NC], F32),
    "t0": ("sbuf", [128, W], BF), "t1": ("sbuf", [128, W], BF),
    "oc": ("sbuf", [128, HEADS * NC], F8), "op": ("sbuf", [128, HEADS * NC], U8),
    "ic": ("sbuf", [128, HEADS * NC], F8), "ip": ("sbuf", [128, HEADS * NC], U8),
    "rc": ("sbuf", [128, ROOM], F8), "rp": ("sbuf", [128, ROOM], U8),
    "ys": ("sbuf", [128, HEADS * NC], F32),
    "ps": ("psum", [128, 8 * BANK], F32),
}
_A = ["lv", "qv", "qo", "ez", "at", "my", "ey", "cin", "pin", "half"]
SEMAPHORES = (["%s%d" % (n, a) for n in _A for a in range(HEADS)]
              + ["%s%d" % (n, i) for n in ("mz", "md", "ed") for i in range(HEADS * G)]
              + ["lk0%d" % i for i in range(G)] + ["qk0%d" % i for i in range(G)]
              + ["lk1%d" % i for i in range(2)] + ["qk1%d" % i for i in range(2)]
              + ["pass%d" % i for i in range(PLACES)]
              + ["lq", "one", "w", "qs", "qq", "st", "loc"])


def engines(topo, src, dst, share):
    m = topo.mask(src, dst)
    bits = [i for i in range(m.bit_length()) if (m >> i) & 1]
    if share and len(bits) > 8:
        bits = bits[0::2] if share == "c" else bits[1::2]
    return sum(1 << i for i in bits)


def count(mask):
    return bin(mask).count("1")


def routes(T, topo):
    cores = T.cores
    crossing = [r for r in range(N - 1) if not topo.may_write(cores[r], cores[r + 1])]

    def near(r):
        src, dst = cores[r], cores[r + 1]
        idle = [c for c in range(128) if topo.chip(c) == topo.chip(src) and topo.may_write(c, dst) and T.rank_of(c) is None]
        return min(idle, key=lambda c: (topo.die(c) != topo.die(src), c))

    def plane(r, s):
        return topo.same_plane(topo.chip(cores[r]), topo.chip(cores[s]))

    out = {}
    for r in range(N - 1):
        for a in range(HEADS):
            if r not in crossing:
                out[r, a] = [("c", 0, NC, (), ""), ("p", 0, NC, (), "")]
                continue
            before, share = cores[r - 1], a == 0
            codes = before if r == crossing[0] else near(r)
            out[r, a] = [("c", 0, NC, (codes,), "c" if share else ""), ("p", 0, NC, (before,), "p" if share else "")]
        if r in crossing and not [s for s in crossing if s < r and plane(r, s)]:
            later = [s for s in crossing if s > r and plane(r, s)]
            ahead = [cores[s] for s in range(r + 3, N - 1) if plane(r, s) and topo.may_write(cores[s], cores[r + 1])]
            there = [cores[s] for s in crossing if s > r and plane(r + 1, s)]
            half = NC // 2
            pieces = [("p", half * i, half, (ahead[i], there[i]), "") for i in range(2)]
            by = []
            for i in range(2):
                by += [near(later[i])] + ahead[2:][::-1][i:i + 1]
            first = 0
            for f, n in zip(by, RUNS[len(by)]):
                pieces.append(("c", first, n, (f,), ""))
                first += n
            out[r, 1] = pieces
    return out


def parts(b):
    return [(0, NC // 2), (NC // 2, NC // 2)] if b == 0 else [(0, NC)]


def rank_program(g, core, T, topo):
    sent = [0]
    COPY = ActivationFunctionType.Copy
    ways = routes(T, topo)
    rank = T.rank_of(core)
    passing, fill = {}, {}
    for key in sorted(ways):
        for j, (kind, first, n, by, share) in enumerate(ways[key]):
            for f in by:
                passing[f, key, j] = (fill.get(f, 0), fill.get((f, kind), 0))
                fill[f] = fill.get(f, 0) + 1
                fill[f, kind] = fill.get((f, kind), 0) + n

    def sem(name):
        return T.sem[name]

    def cols(a):
        return slice(NC * a, NC * a + NC)

    def view(buf, kind, first, n):
        v = T[buf + kind][:, first:first + n]
        return v.bitcast(dt.uint8) if kind == "c" else v

    def stations(key, j):
        return [T.cores[key[0]]] + list(ways[key][j][3]) + [T.cores[key[0] + 1]]

    def write(key, j, step, buf, at):
        r, a = key
        kind, first, n, by, share = ways[key][j]
        dst = stations(key, j)[step + 1]
        if step < len(by):
            place, column = passing[dst, key, j]
            to, s = view("r", kind, column, n), "pass%d" % place
        else:
            to, s = view("i", kind, NC * a + first, n), "%sin%d" % (kind, a)
        rid, pid, _ = topo.addr(dst)
        m = engines(topo, core, dst, share)
        g.remote_dma(to, view(buf, kind, at, n), sem(s), T.sem.loc, pid, rid, m)
        sent[0] += count(m)

    def hand_on(key):
        g.wait_ge(sem("qo%d" % key[1]), 1)
        for j, piece in enumerate(ways[key]):
            write(key, j, 0, "o", NC * key[1] + piece[1])

    def forward(key):
        for j, piece in enumerate(ways[key]):
            if core in piece[3]:
                step = piece[3].index(core) + 1
                place, column = passing[core, key, j]
                g.wait_ge(sem("pass%d" % place), count(engines(topo, stations(key, j)[step - 1], core, piece[4])))
                write(key, j, step, "r", column)

    def arriving(key, kind):
        return sum(count(engines(topo, stations(key, j)[-2], core, p[4])) for j, p in enumerate(ways[key]) if p[0] == kind)

    if rank is not None:
        def kt(i, n=1):
            return slice(W * i, W * (i + n))
        g.sync.dma_start(T.vt[:, 0:W], T.v[:, 0:W]).then_inc(T.sem.lv0, 16)
        for i in range(G):
            queue = g.sync if i % 2 else g.scalar
            queue.dma_start(T.kt[:, kt(i)], T.k[:, kt(i)]).then_inc(sem("lk0%d" % i), 16)
        g.sync.dma_start(T.vt[:, W:2 * W], T.v[:, W:2 * W]).then_inc(T.sem.lv1, 16)
        for i in range(2):
            queue = g.sync if i % 2 else g.scalar
            queue.dma_start(T.kt[:, kt(G + 2 * i, 2)], T.k[:, kt(G + 2 * i, 2)]).then_inc(sem("lk1%d" % i), 16)
        g.sync.dma_start(T.qt[:], T.q[:]).then_inc(T.sem.lq, 16)

        def quantise_q():
            g.vector.wait_ge(T.sem.lq, 16)
            g.vector.quantize_mx(T.qc[:], T.qp[:], T.qt[:]).then_inc(T.sem.qq, 1)

        if rank > 0:
            g.vector.memset(T.one[:], 1.0).then_inc(T.sem.one, 1)
            g.wait_ge(T.sem.one, 1)
            g.affine_select(T.w[:], T.one[:], [[-1, W + 4]], AluOpType.is_equal, 0.0, 3, 4).then_inc(T.sem.w, 1)
        g.vector.wait_ge(T.sem.lv0, 16)
        g.vector.quantize_mx(T.vc[:, cols(0)], T.vp[:, cols(0)], T.vt[:, 0:W]).then_inc(T.sem.qv0, 1)
        for i in range(G):
            g.vector.wait_ge(sem("lk0%d" % i), 16)
            g.vector.quantize_mx(T.kc[:, cols(i)], T.kp[:, cols(i)], T.kt[:, kt(i)]).then_inc(sem("qk0%d" % i), 1)

        def quantise_head1():
            g.vector.wait_ge(T.sem.lv1, 16)
            g.vector.quantize_mx(T.vc[:, cols(1)], T.vp[:, cols(1)], T.vt[:, W:2 * W]).then_inc(T.sem.qv1, 1)
            for i in range(2):
                two = slice(NC * (G + 2 * i), NC * (G + 2 * i + 2))
                g.vector.wait_ge(sem("lk1%d" % i), 16)
                g.vector.quantize_mx(T.kc[:, two], T.kp[:, two], T.kt[:, kt(G + 2 * i, 2)]).then_inc(sem("qk1%d" % i), 1)

        def quantise_state(a, n):
            g.vector.wait_ge(sem("at%d" % a), n)
            g.vector.quantize_mx(T.oc[:, cols(a)], T.op[:, cols(a)], T["t%d" % a][:]).then_inc(sem("qo%d" % a), 1)

        if rank == 0:
            quantise_state(0, G)
            quantise_head1()
            quantise_state(1, G)
            quantise_q()
        else:
            g.vector.wait_ge(T.sem.w, 1)
            for b in range(G):
                g.vector.quantize_mx(T.sc[:, cols(b)], T.sp[:, cols(b)], T.w[:, 3 - b:3 - b + W]).then_inc(T.sem.qs, 1)
            quantise_head1()
            if rank > 1:
                quantise_q()
            g.vector.wait_ge(T.sem.ez0, G)
            g.vector.wait_ge(T.sem.ez1, G)
            for a in range(HEADS):
                made = 0
                for b in range(G):
                    i = G * a + b
                    for first, n in parts(b):
                        g.vector.wait_ge(sem("half%d" % a if n < NC and first == 0 else "ed%d" % i), 1)
                        x = slice(NC * i + first, NC * i + first + n)
                        g.vector.tensor_tensor(T["t%d" % a][:, G * first + b:G * (first + n):G], T.ds[:, x], T.zs[:, x], AluOpType.add).then_inc(sem("at%d" % a), 1)
                        made += 1
                quantise_state(a, made)
            if rank == 1:
                quantise_q()

        def bank(i, first=0, n=NC):
            return T.ps[:, BANK * i + first:BANK * i + first + n]
        for a in range(HEADS):
            g.tensor.wait_ge(sem("qv%d" % a), 1)
            for b in range(G):
                i = G * a + b
                if a == 0:
                    g.tensor.wait_ge(sem("qk0%d" % b), 1)
                elif b % 2 == 0:
                    g.tensor.wait_ge(sem("qk1%d" % (b // 2)), 1)
                g.tensor.matmul_mx(bank(i), T.kc[:, cols(i)], T.kp[:, cols(i)], T.vc[:, cols(a)], T.vp[:, cols(a)], True, True).then_inc(sem("mz%d" % i), 1)
        if rank > 0:
            g.tensor.wait_ge(T.sem.qs, G)
            for a in range(HEADS):
                g.tensor.wait_ge(sem("ez%d" % a), G)
            for a in range(HEADS):
                for kind in ("c", "p"):
                    g.tensor.wait_ge(sem("%sin%d" % (kind, a)), arriving((rank - 1, a), kind))
                for b in range(G):
                    i = G * a + b
                    g.tensor.matmul_mx(bank(i), T.sc[:, cols(b)], T.sp[:, cols(b)], T.ic[:, cols(a)], T.ip[:, cols(a)], True, True).then_inc(sem("md%d" % i), 1)
        for a in range(HEADS):
            g.tensor.wait_ge(sem("qo%d" % a), 1)
            if a == 0:
                g.tensor.wait_ge(T.sem.qq, 1)
            g.tensor.matmul_mx(bank(a), T.oc[:, cols(a)], T.op[:, cols(a)], T.qc[:, cols(a)], T.qp[:, cols(a)], True, True).then_inc(sem("my%d" % a), 1)

        for a in range(HEADS):
            for b in range(G):
                i = G * a + b
                g.scalar.wait_ge(sem("mz%d" % i), 1)
                if rank == 0:
                    g.scalar.activation(T["t%d" % a][:, b:W:G], bank(i), COPY, scale=C).then_inc(sem("at%d" % a), 1)
                else:
                    g.scalar.activation(T.zs[:, cols(i)], bank(i), COPY, scale=C).then_inc(sem("ez%d" % a), 1)
        if rank > 0:
            for a in range(HEADS):
                for b in range(G):
                    i = G * a + b
                    g.scalar.wait_ge(sem("md%d" % i), 1)
                    for first, n in parts(b):
                        done = sem("half%d" % a if n < NC and first == 0 else "ed%d" % i)
                        g.scalar.activation(T.ds[:, NC * i + first:NC * i + first + n], bank(i, first, n), COPY, scale=DEC).then_inc(done, 1)
        for a in range(HEADS):
            g.scalar.wait_ge(sem("my%d" % a), 1)
            g.scalar.activation(T.ys[:, cols(a)], bank(a), COPY).then_inc(sem("ey%d" % a), 1)

        for a in range(HEADS):
            g.sync.wait_ge(sem("ey%d" % a), 1)
            g.sync.dma_start(T.y[:, cols(a)], T.ys[:, cols(a)]).then_inc(T.sem.st, 16)
        g.sync.wait_ge(T.sem.st, 16 * HEADS)

    for key in sorted(ways):
        if key[0] == rank:
            hand_on(key)
        else:
            forward(key)
    if sent[0]:
        g.wait_ge(T.sem.loc, sent[0])
